import numpy as np
import ml_dtypes

BF16 = ml_dtypes.bfloat16


def bf(x):
    return np.asarray(x, np.float32).astype(BF16)


def f32(x):
    return np.asarray(x, np.float32)


def f64(x):
    return np.asarray(x).astype(np.float64)


def striped(idx):
    return np.concatenate([l.reshape(-1, 16).T for l in idx])


def rows(idx, k):
    return np.tile(np.repeat(idx, 16, axis=0), (k // (16 * 8), 1))


def look(tab, idx):
    return np.take_along_axis(f64(tab), rows(idx, len(tab)), axis=1)


K, S, V, N, M = 512, 2048, 1024, 1024, 128


def setup_inputs():
    return {"tab": f32(np.random.standard_normal((K, S))), "qry": f32(np.random.standard_normal((K, V))), "w": bf(np.random.uniform(0.0, 2.0, (K, M)) / K), "offs": striped(np.random.randint(0, S, (8, N)))}


def reference(tab, qry, w, offs):
    idx = np.stack([g.T.reshape(-1) for g in np.split(offs, 8)])
    x = (look(tab, idx) - f64(qry)) ** 2
    y = f64(w).T @ x
    return y

@@ -1,0 +1,56 @@
+import concourse.mybir as mybir
+
+P = 128
+K, S, N, M = 512, 2048, 1024, 128
+BLOCKS = K // P
+PIECE = 512
+PIECES = N // PIECE
+LIST_COLUMNS = PIECE // 16
+
+FLOPS = 2 * K * M * N + 2 * K * N
+
+F32, BF16, U16 = mybir.dt.float32, mybir.dt.bfloat16, mybir.dt.uint16
+SUBTRACT = mybir.AluOpType.subtract
+SQUARE = mybir.ActivationFunctionType.Square
+
+
+def tile_lookup_dist_sub_none_kernel(tc, tab, qry, w, offs, out):
+    nc = tc.nc
+    tab_blocks = tab.rearrange("(b p) s -> b p s", p=P)
+    qry_blocks = qry.rearrange("(b p) n -> b p n", p=P)
+    with (
+        tc.tile_pool(name="held", bufs=1) as held,
+        tc.tile_pool(name="work", bufs=3) as work,
+        tc.psum_pool(name="psum", bufs=1) as psum,
+    ):
+        lists = held.tile([P, N // 16], U16, name="lists")
+        nc.sync.dma_start(lists[:], offs)
+        weights = held.tile([P, BLOCKS, M], BF16, name="weights")
+        nc.scalar.dma_start(weights[:], w.rearrange("(b p) m -> p b m", p=P))
+
+        windows, queries = [], []
+        for b in range(BLOCKS):
+            window = held.tile([P, S], F32, name=f"window{b}")
+            query = held.tile([P, N], F32, name=f"query{b}")
+            nc.sync.dma_start(window[:], tab_blocks[b])
+            nc.sync.dma_start(query[:], qry_blocks[b])
+            windows.append(window)
+            queries.append(query)
+
+        sums = [psum.tile([P, PIECE], F32, name=f"sum{c}") for c in range(PIECES)]
+        for b in range(BLOCKS):
+            for c in range(PIECES):
+                columns = slice(c * PIECE, (c + 1) * PIECE)
+                picked = windows[b][:].indirect(lists[:, c * LIST_COLUMNS : (c + 1) * LIST_COLUMNS])
+                difference = work.tile([P, PIECE], F32, name="difference")
+                nc.vector.tensor_tensor(difference[:], picked, queries[b][:, columns], SUBTRACT)
+                squared = work.tile([P, PIECE], BF16, name="squared")
+                nc.scalar.activation(squared[:], difference[:], SQUARE)
+                nc.tensor.matmul(
+                    sums[c][:], weights[:, b, :], squared[:], start=(b == 0), stop=(b == BLOCKS - 1)
+                )
+
+        for c in range(PIECES):
+            result = held.tile([P, PIECE], F32, name=f"result{c}")
+            nc.vector.tensor_copy(result[:], sums[c][:])
+            nc.sync.dma_start(out[:, c * PIECE : (c + 1) * PIECE], result[:])

@@ -4,6 +4,8 @@ P = 128
 K, S, N, M = 512, 2048, 1024, 128
 BLOCKS = K // P
 PIECE = 512
+CHUNK = 256
+BANK = 512
 PIECES = N // PIECE
 LIST_COLUMNS = PIECE // 16
 
@@ -26,31 +28,35 @@ def tile_lookup_dist_sub_none_kernel(tc, tab, qry, w, offs, out):
         lists = held.tile([P, N // 16], U16, name="lists")
         nc.sync.dma_start(lists[:], offs)
         weights = held.tile([P, BLOCKS, M], BF16, name="weights")
-        nc.scalar.dma_start(weights[:], w.rearrange("(b p) m -> p b m", p=P))
 
         windows, queries = [], []
         for b in range(BLOCKS):
             window = held.tile([P, S], F32, name=f"window{b}")
-            query = held.tile([P, N], F32, name=f"query{b}")
             nc.sync.dma_start(window[:], tab_blocks[b])
-            nc.sync.dma_start(query[:], qry_blocks[b])
             windows.append(window)
-            queries.append(query)
+            for c in range(PIECES):
+                query = held.tile([P, PIECE], F32, name=f"query{b}_{c}")
+                nc.sync.dma_start(query[:], qry_blocks[b][:, c * PIECE : (c + 1) * PIECE])
+                queries.append(query)
+            if b == 0:
+                nc.sync.dma_start(weights[:], w.rearrange("(b p) m -> p b m", p=P))
 
-        sums = [psum.tile([P, PIECE], F32, name=f"sum{c}") for c in range(PIECES)]
+        sums = [psum.tile([P, BANK], F32, name=f"sum{i}") for i in range(N // CHUNK)]
         for b in range(BLOCKS):
             for c in range(PIECES):
-                columns = slice(c * PIECE, (c + 1) * PIECE)
                 picked = windows[b][:].indirect(lists[:, c * LIST_COLUMNS : (c + 1) * LIST_COLUMNS])
                 difference = work.tile([P, PIECE], F32, name="difference")
-                nc.vector.tensor_tensor(difference[:], picked, queries[b][:, columns], SUBTRACT)
-                squared = work.tile([P, PIECE], BF16, name="squared")
-                nc.scalar.activation(squared[:], difference[:], SQUARE)
-                nc.tensor.matmul(
-                    sums[c][:], weights[:, b, :], squared[:], start=(b == 0), stop=(b == BLOCKS - 1)
-                )
+                nc.vector.tensor_tensor(difference[:], picked, queries[b * PIECES + c][:], SUBTRACT)
+                for h in range(PIECE // CHUNK):
+                    part = slice(h * CHUNK, (h + 1) * CHUNK)
+                    total = sums[c * (PIECE // CHUNK) + h][:, :CHUNK]
+                    squared = work.tile([P, CHUNK], BF16, name="squared")
+                    nc.scalar.activation(squared[:], difference[:, part], SQUARE)
+                    nc.tensor.matmul(
+                        total, weights[:, b, :], squared[:], start=(b == 0), stop=(b == BLOCKS - 1)
+                    )
 
-        for c in range(PIECES):
-            result = held.tile([P, PIECE], F32, name=f"result{c}")
-            nc.vector.tensor_copy(result[:], sums[c][:])
-            nc.sync.dma_start(out[:, c * PIECE : (c + 1) * PIECE], result[:])
+        for i in range(N // CHUNK):
+            result = held.tile([P, CHUNK], F32, name=f"result{i}")
+            nc.vector.tensor_copy(result[:], sums[i][:, :CHUNK])
+            nc.sync.dma_start(out[:, i * CHUNK : (i + 1) * CHUNK], result[:])

@@ -34,10 +34,11 @@ def tile_lookup_dist_sub_none_kernel(tc, tab, qry, w, offs, out):
             window = held.tile([P, S], F32, name=f"window{b}")
             nc.sync.dma_start(window[:], tab_blocks[b])
             windows.append(window)
-            for c in range(PIECES):
-                query = held.tile([P, PIECE], F32, name=f"query{b}_{c}")
-                nc.sync.dma_start(query[:], qry_blocks[b][:, c * PIECE : (c + 1) * PIECE])
-                queries.append(query)
+            width = PIECE if b == BLOCKS - 1 else N
+            for first in range(0, N, width):
+                query = held.tile([P, width], F32, name=f"query{b}_{first}")
+                nc.sync.dma_start(query[:], qry_blocks[b][:, first : first + width])
+                queries += [query[:, c : c + PIECE] for c in range(0, width, PIECE)]
             if b == 0:
                 nc.sync.dma_start(weights[:], w.rearrange("(b p) m -> p b m", p=P))
 
@@ -46,7 +47,7 @@ def tile_lookup_dist_sub_none_kernel(tc, tab, qry, w, offs, out):
             for c in range(PIECES):
                 picked = windows[b][:].indirect(lists[:, c * LIST_COLUMNS : (c + 1) * LIST_COLUMNS])
                 difference = work.tile([P, PIECE], F32, name="difference")
-                nc.vector.tensor_tensor(difference[:], picked, queries[b * PIECES + c][:], SUBTRACT)
+                nc.vector.tensor_tensor(difference[:], picked, queries[b * PIECES + c], SUBTRACT)
                 for h in range(PIECE // CHUNK):
                     part = slice(h * CHUNK, (h + 1) * CHUNK)
                     total = sums[c * (PIECE // CHUNK) + h][:, :CHUNK]

import concourse.mybir as mybir

P = 128
K, S, N, M = 512, 2048, 1024, 128
BLOCKS = K // P
PIECE = 512
CHUNK = 256
BANK = 512
PIECES = N // PIECE
LIST_COLUMNS = PIECE // 16

FLOPS = 2 * K * M * N + 2 * K * N

F32, BF16, U16 = mybir.dt.float32, mybir.dt.bfloat16, mybir.dt.uint16
SUBTRACT = mybir.AluOpType.subtract
SQUARE = mybir.ActivationFunctionType.Square


def tile_lookup_dist_sub_none_kernel(tc, tab, qry, w, offs, out):
    nc = tc.nc
    tab_blocks = tab.rearrange("(b p) s -> b p s", p=P)
    qry_blocks = qry.rearrange("(b p) n -> b p n", p=P)
    with (
        tc.tile_pool(name="held", bufs=1) as held,
        tc.tile_pool(name="work", bufs=3) as work,
        tc.psum_pool(name="psum", bufs=1) as psum,
    ):
        lists = held.tile([P, N // 16], U16, name="lists")
        nc.sync.dma_start(lists[:], offs)
        weights = held.tile([P, BLOCKS, M], BF16, name="weights")

        windows, queries = [], []
        for b in range(BLOCKS):
            window = held.tile([P, S], F32, name=f"window{b}")
            nc.sync.dma_start(window[:], tab_blocks[b])
            windows.append(window)
            width = PIECE if b == BLOCKS - 1 else N
            for first in range(0, N, width):
                query = held.tile([P, width], F32, name=f"query{b}_{first}")
                nc.sync.dma_start(query[:], qry_blocks[b][:, first : first + width])
                queries += [query[:, c : c + PIECE] for c in range(0, width, PIECE)]
            if b == 0:
                nc.sync.dma_start(weights[:], w.rearrange("(b p) m -> p b m", p=P))

        sums = [psum.tile([P, BANK], F32, name=f"sum{i}") for i in range(N // CHUNK)]
        for b in range(BLOCKS):
            for c in range(PIECES):
                picked = windows[b][:].indirect(lists[:, c * LIST_COLUMNS : (c + 1) * LIST_COLUMNS])
                difference = work.tile([P, PIECE], F32, name="difference")
                nc.vector.tensor_tensor(difference[:], picked, queries[b * PIECES + c], SUBTRACT)
                for h in range(PIECE // CHUNK):
                    part = slice(h * CHUNK, (h + 1) * CHUNK)
                    total = sums[c * (PIECE // CHUNK) + h][:, :CHUNK]
                    squared = work.tile([P, CHUNK], BF16, name="squared")
                    nc.scalar.activation(squared[:], difference[:, part], SQUARE)
                    nc.tensor.matmul(
                        total, weights[:, b, :], squared[:], start=(b == 0), stop=(b == BLOCKS - 1)
                    )

        for i in range(N // CHUNK):
            result = held.tile([P, CHUNK], F32, name=f"result{i}")
            nc.vector.tensor_copy(result[:], sums[i][:, :CHUNK])
            nc.sync.dma_start(out[:, i * CHUNK : (i + 1) * CHUNK], result[:])
